import numpy as np
import ml_dtypes


def mxq(x, axis, fmt="e4m3"):
    dtype, down = {"e4m3": (ml_dtypes.float8_e4m3fn, 7), "e5m2": (ml_dtypes.float8_e5m2, 14)}[fmt]
    v = np.moveaxis(np.asarray(x, np.float32).astype(ml_dtypes.bfloat16).astype(np.float64), axis, -1)
    blocks = v.reshape(v.shape[:-1] + (-1, 32))
    amax = np.abs(blocks).max(-1, keepdims=True)
    byte = np.maximum(np.where(amax > 0, np.frexp(amax)[1] - 1 + 127, 0) - down, 1)
    scale = np.exp2(byte - 127.0)
    codes = (blocks / scale).astype(np.float32).astype(dtype).astype(np.float64)
    return np.moveaxis((codes * scale).reshape(v.shape), -1, axis)


WIDE = False


def mx_kscale(k):
    if not WIDE:
        return np.ones(k)
    levels = np.array([10, -10, 5, -5, 0])
    if k % 512:
        return np.exp2(np.random.permutation(np.resize(levels, k // 32))).repeat(32)
    a = np.empty((k // 512, 16))
    for p in range(k // 512):
        a[p, :8] = np.random.permutation(np.resize(levels, 8))
        for g in range(8):
            far = levels[np.abs(levels - a[p, g]) >= 10]
            a[p, g + 8] = far[np.random.randint(len(far))]
    return np.exp2(a.ravel()).repeat(32)


def f64(x):
    return np.asarray(x).astype(np.float64)


def striped(idx):
    return np.tile(np.asarray(idx).reshape(-1, 16).T, (8, 1)).astype(np.uint16)


def unstriped(offs):
    return offs[:16].T.reshape(-1).astype(np.int64)


E2M1 = np.array([0.0, 0.5, 1.0, 1.5, 2.0, 3.0, 4.0, 6.0, -0.0, -0.5, -1.0, -1.5, -2.0, -3.0, -4.0, -6.0])


def pack_weight(w, fmt):
    k, n = w.shape
    w = f64(np.asarray(w, np.float32).astype(ml_dtypes.bfloat16)).reshape(k // 32, 32, n)
    amax = np.abs(w).max(1)
    if fmt == "e4m3":
        byte = np.frexp(amax)[1] - 1 + 127 - 7
    else:
        mant, ex = np.frexp(amax / 6.0)
        byte = np.where(mant > 0.5, ex, ex - 1) + 127
    byte = np.clip(np.where(amax > 0, byte, 1), 1, 254)
    scaled = (w * np.exp2(127.0 - byte)[:, None, :]).reshape(k, n).astype(np.float32)
    by_word = np.ascontiguousarray(scaled.reshape(k // 512, 128, 4, n).transpose(0, 1, 3, 2))
    if fmt == "e4m3":
        words = by_word.astype(ml_dtypes.float8_e4m3fn).view(np.uint8)
    else:
        c = by_word.astype(ml_dtypes.float4_e2m1fn).view(np.uint8) & 0xF
        words = (c[..., 0::2] | (c[..., 1::2] << 4)).reshape(k // 512, 128, 2 * n)
    return np.ascontiguousarray(words), np.ascontiguousarray(byte.astype(np.uint8).reshape(k // 512, 16, n))


def unpack_weight(words, scales, fmt):
    g, _, n = scales.shape
    words = np.ascontiguousarray(words).reshape(g, 128, n, -1)
    if fmt == "e4m3":
        vals = words.view(ml_dtypes.float8_e4m3fn).astype(np.float64)
    else:
        nib = np.empty((g, 128, n, 4), np.uint8)
        nib[..., 0::2] = words & 0xF
        nib[..., 1::2] = words >> 4
        vals = E2M1[nib]
    vals = vals * np.repeat(np.exp2(scales.astype(np.float64) - 127.0), 8, axis=1)[..., None]
    return vals.transpose(0, 1, 3, 2).reshape(g * 512, n)


def sigmoid(v):
    return 1.0 / (1.0 + np.exp(-v))


D, E, T, I, Q, G = 512, 512, 2048, 512, 128, 64


def setup_inputs():
    n = np.random.standard_normal
    idx = np.random.permutation(T)[:I]
    fd = mx_kscale(D)
    fi = mx_kscale(I)
    ti = np.ones(T)
    ti[idx] = fi
    keysp = pack_weight(n((D, T)) / fd[:, None], "e4m3")
    return {
        "query": (n((D, Q)) * 0.6 / np.sqrt(D) * fd[:, None]).astype(np.float32),
        "dquery": (n((D, Q)) * 1.0 / np.sqrt(D) * fd[:, None]).astype(np.float32),
        "keys_words": keysp[0],
        "keys_scales": keysp[1],
        "os": (np.random.uniform(1.0, 4.0, (1, I)) * fi).astype(np.float32),
        "vals": (n((E, T)) / ti).astype(np.float32),
        "offs": striped(idx),
    }


def reference(query, dquery, keys_words, keys_scales, os, vals, offs):
    idx = unstriped(offs)
    keysu = unpack_weight(keys_words, keys_scales, "e4m3")
    queryq = mxq(f64(query), 0, "e4m3")
    keysidxg = keysu[:, idx]
    a = queryq.T @ keysidxg
    dqueryq = mxq(f64(dquery), 0, "e4m3")
    ta = dqueryq.T @ keysidxg
    s = a.reshape(Q, G, I // G).mean(axis=2)
    p = np.exp(s - np.max(s, axis=1, keepdims=True))
    r = p / np.sum(p, axis=1, keepdims=True)
    rr = np.repeat(r, I // G, axis=1)
    ts = ta.reshape(Q, G, I // G).mean(axis=2)
    tp = ts * p
    tr = (tp - np.sum(tp, axis=1, keepdims=True) * p / np.sum(p, axis=1, keepdims=True)) / np.sum(p, axis=1, keepdims=True)
    trr = np.repeat(tr, I // G, axis=1)
    tw = trr * sigmoid(a) + ta * sigmoid(a) * (1.0 - sigmoid(a)) * rr
    wo1 = tw * f64(os)
    wt1 = wo1.T
    vt1 = f64(vals)[:, idx].T
    wt1q = mxq(wt1, 0, "e4m3")
    vt1q = mxq(vt1, 0, "e4m3")
    o = wt1q.T @ vt1q
    return o

@@ -1,0 +1,185 @@
+from contextlib import ExitStack
+
+import concourse.mybir as mybir
+from concourse.masks import make_identity
+
+D, E, T, SLOTS, Q, SPANS = 512, 512, 2048, 512, 128, 64
+SPAN = SLOTS // SPANS
+FLOPS = 2 * Q * SLOTS * D * 2 + 2 * Q * SLOTS * E
+
+F32 = mybir.dt.float32
+BF16 = mybir.dt.bfloat16
+I32 = mybir.dt.int32
+U32 = mybir.dt.uint32
+U16 = mybir.dt.uint16
+U8 = mybir.dt.uint8
+FP8X4 = mybir.dt.float8_e4m3fn_x4
+ALU = mybir.AluOpType
+ACT = mybir.ActivationFunctionType
+AXIS = mybir.AxisListType
+
+P = 128
+PACK = 4
+BLOCKS = E // P
+HALVES = 2
+HALF = SLOTS // HALVES
+
+
+def tile_attend_ttspanread_kernel(tc, query, dquery, keys_words, keys_scales, slot_factor, vals, offs, out):
+    nc = tc.nc
+    with ExitStack() as ctx:
+        sb = ctx.enter_context(tc.tile_pool(name="sb", bufs=1))
+        ps = ctx.enter_context(tc.psum_pool(name="ps", bufs=1))
+        ps_v = ctx.enter_context(tc.psum_pool(name="ps_v", bufs=2))
+
+        def in_slot(slot, shape, dtype, name):
+            return sb.tile(shape, dtype, name=name, tag=slot, align_bytes=64)
+
+        offsets = sb.tile([P, SLOTS // 16], U16, name="offsets")
+        key_bytes = in_slot("slot_b", [P, T], U8, "key_bytes")
+        nc.gpsimd.memset(key_bytes[:].bitcast(I32), 0)
+        identity = sb.tile([P, P], F32, name="identity")
+        make_identity(nc, identity[:])
+
+        q_raw = in_slot("slot_q", [P, PACK, Q], F32, "q_raw")
+        dq_raw = in_slot("slot_dq", [P, PACK, Q], F32, "dq_raw")
+        key_words = in_slot("slot_k", [P, T], U32, "key_words")
+        nc.sync.dma_start(offsets[:], offs)
+        nc.sync.dma_start(q_raw[:], query.rearrange("(p j) q -> p j q", j=PACK))
+        nc.sync.dma_start(dq_raw[:], dquery.rearrange("(p j) q -> p j q", j=PACK))
+        for quad in range(4):
+            nc.scalar.dma_start(
+                key_bytes[32 * quad : 32 * quad + 4, :].bitcast(I32),
+                keys_scales[0, 4 * quad : 4 * quad + 4, :].bitcast(I32),
+            )
+        nc.sync.dma_start(key_words[:].bitcast(I32), keys_words[0].rearrange("p n t -> p (n t)").bitcast(I32))
+        pools = {}
+
+        def load_values(b, slot):
+            pools[b] = in_slot(slot, [P, T], F32, f"vals{b}")
+            nc.sync.dma_start(pools[b][:], vals[b * P : (b + 1) * P, :])
+
+        def quantize_rows(raw, name, round_rows):
+            rounded = in_slot(name + "_bf", [P, Q, PACK], BF16, name + "_bf")
+            round_rows(rounded[:], raw[:].rearrange("p j q -> p q j"))
+            codes = sb.tile([P, Q], U32, name=name + "_codes", align_bytes=64)
+            scales = sb.tile([P, Q], U8, name=name + "_scales", align_bytes=64)
+            nc.vector.quantize_mx(out=codes[:].bitcast(FP8X4), scales=scales[:], in_=rounded[:].rearrange("p q j -> p (q j)"))
+            return codes, scales
+
+        got_bytes = sb.tile([P, SLOTS], U8, name="got_bytes", align_bytes=64)
+        nc.vector.tensor_copy(got_bytes[:], key_bytes[:].indirect(offsets[:]))
+        q_mx = quantize_rows(q_raw, "q", nc.vector.tensor_copy)
+        load_values(0, "slot_q")
+        dq_mx = quantize_rows(dq_raw, "dq", lambda dst, src: nc.scalar.activation(dst, src, ACT.Copy))
+        load_values(1, "slot_dq")
+        load_values(2, "dq_bf")
+        factor = in_slot("q_bf", [P, PACK], F32, "factor")
+        nc.sync.dma_start(factor[:], slot_factor.rearrange("o (p t) -> p (o t)", t=PACK))
+
+        scores = []
+        all_words = in_slot("slot_b", [P, SLOTS], U32, "got_words")
+        for h in range(HALVES):
+            got_words = all_words[:, h * HALF : (h + 1) * HALF]
+            nc.vector.tensor_copy(got_words, key_words[:].indirect(offsets[:, h * HALF // 16 : (h + 1) * HALF // 16]))
+            bank = ps.tile([P, 2, HALF], F32, name=f"scores{h}")
+            for c, (codes, scales) in enumerate((q_mx, dq_mx)):
+                nc.tensor.matmul_mx(
+                    out=bank[:, c, :], lhsT=codes[:].bitcast(FP8X4), lhsT_scale=scales[:],
+                    rhs=got_words.bitcast(FP8X4), rhs_scale=got_bytes[:, h * HALF : (h + 1) * HALF], start=True, stop=True,
+                )
+            scores.append(bank)
+        load_values(3, "slot_k")
+
+        sums = sb.tile([P, 2, SPANS], F32, name="sums")
+        sig = sb.tile([P, SLOTS], F32, name="sig")
+        nsig = sb.tile([P, SLOTS], F32, name="nsig")
+        for h in range(HALVES):
+            nc.vector.tensor_reduce(
+                sums[:, :, h * SPANS // HALVES : (h + 1) * SPANS // HALVES],
+                scores[h][:].rearrange("p c (g s) -> p c g s", s=SPAN), AXIS.X, ALU.add,
+            )
+            nc.scalar.activation(nsig[:, h * HALF : (h + 1) * HALF], scores[h][:, 0, :], ACT.Sigmoid, scale=-1.0)
+            nc.scalar.activation(sig[:, h * HALF : (h + 1) * HALF], scores[h][:, 0, :], ACT.Sigmoid)
+        a_sum, ta_sum = sums[:, 0, :], sums[:, 1, :]
+        neg_s = sb.tile([P, SPANS], F32, name="neg_s")
+        neg_max = sb.tile([P, 1], F32, name="neg_max")
+        nc.vector.tensor_scalar(neg_s[:], a_sum, -1.0 / SPAN, None, ALU.mult, ALU.min, accum_out=neg_max[:])
+        p = sb.tile([P, SPANS], F32, name="p")
+        p_sum = sb.tile([P, 1], F32, name="p_sum")
+        nc.scalar.activation(p[:], neg_s[:], ACT.Exp, bias=neg_max[:], scale=-1.0, accum_out=p_sum[:])
+        x = sb.tile([P, SLOTS], F32, name="x")
+        for h in range(HALVES):
+            nc.vector.tensor_tensor(x[:, h * HALF : (h + 1) * HALF], scores[h][:, 1, :], nsig[:, h * HALF : (h + 1) * HALF], ALU.mult)
+
+        def gather_values(b):
+            got = sb.tile([P, SLOTS], BF16, name=f"got_vals{b}")
+            nc.vector.tensor_copy(got[:], pools[b][:].indirect(offsets[:]))
+            pairs = got[:].bitcast(F32)
+            turned = ps_v.tile([P, 2, P], F32, name="turned")
+            for u in range(2):
+                nc.tensor.transpose(turned[:, u, :], pairs[:, u : SLOTS // 2 : 2], identity[:])
+            woven = sb.tile([P, P * PACK], BF16, name=f"woven{b}", align_bytes=64)
+            nc.scalar.copy(woven[:].bitcast(F32).rearrange("p (e u) -> p e u", u=2), turned[:].rearrange("p u e -> p e u"))
+            return woven
+
+        woven = [gather_values(0)]
+        work = in_slot("slot_q", [P, SLOTS + SPANS + 16], F32, "work")
+        y, tp = work[:, 0:SLOTS], work[:, SLOTS : SLOTS + SPANS]
+        inv_sum, tp_sum = work[:, SLOTS + SPANS : SLOTS + SPANS + 1], work[:, SLOTS + SPANS + 8 : SLOTS + SPANS + 9]
+        nc.vector.scalar_tensor_tensor(
+            y.rearrange("p (g s) -> p g s", s=SPAN), ta_sum.unsqueeze(2).to_broadcast([P, SPANS, SPAN]), 1.0 / SPAN,
+            x[:].rearrange("p (g s) -> p g s", s=SPAN), ALU.mult, ALU.add,
+        )
+        nc.vector.reciprocal(inv_sum, p_sum[:])
+        nc.vector.scalar_tensor_tensor(tp, p[:], 1.0 / SPAN, ta_sum, ALU.mult, ALU.mult, accum_out=tp_sum)
+        mean = sb.tile([P, 1], F32, name="mean")
+        nc.scalar.activation(mean[:], tp_sum, ACT.Copy, scale=inv_sum)
+        share = sb.tile([P, SPANS, 2], F32, name="share")
+        nc.scalar.activation(share[:], p[:].unsqueeze(2).to_broadcast([P, SPANS, 2]), ACT.Copy, scale=inv_sum)
+        woven.append(gather_values(1))
+        z = in_slot("slot_dq", [P, SLOTS], F32, "z")
+        nc.vector.scalar_tensor_tensor(z[:], y, mean[:], sig[:], ALU.subtract, ALU.mult)
+
+        share_t = ps.tile([P, Q], F32, name="share_t")
+        nc.tensor.transpose(share_t[:], share[:].rearrange("p g h -> p (g h)"), identity[:])
+        weight = sb.tile([P, PACK, Q], F32, name="weight")
+        for t in range(PACK):
+            nc.scalar.activation(weight[:, t, :], share_t[:], ACT.Copy, scale=factor[:, t : t + 1])
+        z_t = ps.tile([P, PACK, Q], F32, name="z_t")
+        for t in range(PACK):
+            nc.tensor.transpose(z_t[:, t, :], z[:, t:SLOTS:PACK], identity[:])
+        woven.append(gather_values(2))
+        w_bf = in_slot("dq_bf", [P, Q, PACK], BF16, "w_bf")
+        nc.vector.tensor_tensor(w_bf[:], z_t[:].rearrange("p t q -> p q t"), weight[:].rearrange("p t q -> p q t"), ALU.mult)
+        w_codes = sb.tile([P, Q], U32, name="w_codes", align_bytes=64)
+        w_scales = sb.tile([P, Q], U8, name="w_scales", align_bytes=64)
+        nc.vector.quantize_mx(out=w_codes[:].bitcast(FP8X4), scales=w_scales[:], in_=w_bf[:].rearrange("p q t -> p (q t)"))
+        woven.append(gather_values(3))
+
+        v_codes = in_slot("slot_k", [P, E - P], U32, "v_codes")
+        v_scales = sb.tile([P, E - P], U8, name="v_scales", align_bytes=64)
+        v_codes_last = sb.tile([P, P], U32, name="v_codes_last", align_bytes=64)
+        v_scales_last = sb.tile([P, P], U8, name="v_scales_last", align_bytes=64)
+        for b in range(BLOCKS - 1):
+            nc.vector.quantize_mx(out=v_codes[:, b * P : (b + 1) * P].bitcast(FP8X4), scales=v_scales[:, b * P : (b + 1) * P], in_=woven[b][:])
+        nc.vector.quantize_mx(out=v_codes_last[:].bitcast(FP8X4), scales=v_scales_last[:], in_=woven[BLOCKS - 1][:])
+
+        def product(bank, codes, scales):
+            nc.tensor.matmul_mx(
+                out=bank, lhsT=w_codes[:].bitcast(FP8X4), lhsT_scale=w_scales[:],
+                rhs=codes.bitcast(FP8X4), rhs_scale=scales, start=True, stop=True,
+            )
+
+        o_first = ps.tile([P, E - P], F32, name="o_first")
+        product(o_first[:, 0 : 2 * P], v_codes[:, 0 : 2 * P], v_scales[:, 0 : 2 * P])
+        product(o_first[:, 2 * P : 3 * P], v_codes[:, 2 * P : 3 * P], v_scales[:, 2 * P : 3 * P])
+        res_first = sb.tile([P, E - P], F32, name="res_first")
+        nc.scalar.copy(res_first[:], o_first[:])
+        nc.sync.dma_start(out[:, 0 : E - P], res_first[:])
+
+        o_last = ps.tile([P, P], F32, name="o_last")
+        product(o_last[:], v_codes_last[:], v_scales_last[:])
+        res_last = sb.tile([P, P], F32, name="res_last")
+        nc.vector.tensor_copy(res_last[:], o_last[:])
+        nc.sync.dma_start(out[:, E - P : E], res_last[:])

@@ -23,6 +23,7 @@ PACK = 4
 BLOCKS = E // P
 HALVES = 2
 HALF = SLOTS // HALVES
+LINE = 4
 
 
 def tile_attend_ttspanread_kernel(tc, query, dquery, keys_words, keys_scales, slot_factor, vals, offs, out):
@@ -36,7 +37,7 @@ def tile_attend_ttspanread_kernel(tc, query, dquery, keys_words, keys_scales, sl
             return sb.tile(shape, dtype, name=name, tag=slot, align_bytes=64)
 
         offsets = sb.tile([P, SLOTS // 16], U16, name="offsets")
-        key_bytes = in_slot("slot_b", [P, T], U8, "key_bytes")
+        key_bytes = sb.tile([P, T], U8, name="key_bytes")
         nc.gpsimd.memset(key_bytes[:].bitcast(I32), 0)
         identity = sb.tile([P, P], F32, name="identity")
         make_identity(nc, identity[:])
@@ -48,7 +49,7 @@ def tile_attend_ttspanread_kernel(tc, query, dquery, keys_words, keys_scales, sl
         nc.sync.dma_start(q_raw[:], query.rearrange("(p j) q -> p j q", j=PACK))
         nc.sync.dma_start(dq_raw[:], dquery.rearrange("(p j) q -> p j q", j=PACK))
         for quad in range(4):
-            nc.scalar.dma_start(
+            nc.sync.dma_start(
                 key_bytes[32 * quad : 32 * quad + 4, :].bitcast(I32),
                 keys_scales[0, 4 * quad : 4 * quad + 4, :].bitcast(I32),
             )
@@ -61,14 +62,13 @@ def tile_attend_ttspanread_kernel(tc, query, dquery, keys_words, keys_scales, sl
 
         def quantize_rows(raw, name, round_rows):
             rounded = in_slot(name + "_bf", [P, Q, PACK], BF16, name + "_bf")
-            round_rows(rounded[:], raw[:].rearrange("p j q -> p q j"))
+            round_rows(rounded[:].rearrange("p (c i) j -> p c j i", i=LINE), raw[:].rearrange("p j (c i) -> p c j i", i=LINE))
             codes = sb.tile([P, Q], U32, name=name + "_codes", align_bytes=64)
             scales = sb.tile([P, Q], U8, name=name + "_scales", align_bytes=64)
             nc.vector.quantize_mx(out=codes[:].bitcast(FP8X4), scales=scales[:], in_=rounded[:].rearrange("p q j -> p (q j)"))
             return codes, scales
 
         got_bytes = sb.tile([P, SLOTS], U8, name="got_bytes", align_bytes=64)
-        nc.vector.tensor_copy(got_bytes[:], key_bytes[:].indirect(offsets[:]))
         q_mx = quantize_rows(q_raw, "q", nc.vector.tensor_copy)
         load_values(0, "slot_q")
         dq_mx = quantize_rows(dq_raw, "dq", lambda dst, src: nc.scalar.activation(dst, src, ACT.Copy))
@@ -77,69 +77,75 @@ def tile_attend_ttspanread_kernel(tc, query, dquery, keys_words, keys_scales, sl
         factor = in_slot("q_bf", [P, PACK], F32, "factor")
         nc.sync.dma_start(factor[:], slot_factor.rearrange("o (p t) -> p (o t)", t=PACK))
 
+        got_words = sb.tile([P, SLOTS], U32, name="got_words", align_bytes=64)
+        nc.vector.tensor_copy(got_words[:], key_words[:].indirect(offsets[:]))
         scores = []
-        all_words = in_slot("slot_b", [P, SLOTS], U32, "got_words")
         for h in range(HALVES):
-            got_words = all_words[:, h * HALF : (h + 1) * HALF]
-            nc.vector.tensor_copy(got_words, key_words[:].indirect(offsets[:, h * HALF // 16 : (h + 1) * HALF // 16]))
+            cols = slice(h * HALF, (h + 1) * HALF)
+            nc.vector.tensor_copy(got_bytes[:, cols], key_bytes[:].indirect(offsets[:, h * HALF // 16 : (h + 1) * HALF // 16]))
             bank = ps.tile([P, 2, HALF], F32, name=f"scores{h}")
             for c, (codes, scales) in enumerate((q_mx, dq_mx)):
                 nc.tensor.matmul_mx(
                     out=bank[:, c, :], lhsT=codes[:].bitcast(FP8X4), lhsT_scale=scales[:],
-                    rhs=got_words.bitcast(FP8X4), rhs_scale=got_bytes[:, h * HALF : (h + 1) * HALF], start=True, stop=True,
+                    rhs=got_words[:, cols].bitcast(FP8X4), rhs_scale=got_bytes[:, cols], start=True, stop=True,
                 )
             scores.append(bank)
         load_values(3, "slot_k")
 
+        def dealt(scores_half):
+            return scores_half.rearrange("p (m t) -> p t m", t=PACK)
+
         sums = sb.tile([P, 2, SPANS], F32, name="sums")
-        sig = sb.tile([P, SLOTS], F32, name="sig")
-        nsig = sb.tile([P, SLOTS], F32, name="nsig")
+        sig = sb.tile([P, PACK, P], F32, name="sig")
+        part = [slice(h * P // HALVES, (h + 1) * P // HALVES) for h in range(HALVES)]
         for h in range(HALVES):
             nc.vector.tensor_reduce(
                 sums[:, :, h * SPANS // HALVES : (h + 1) * SPANS // HALVES],
                 scores[h][:].rearrange("p c (g s) -> p c g s", s=SPAN), AXIS.X, ALU.add,
             )
-            nc.scalar.activation(nsig[:, h * HALF : (h + 1) * HALF], scores[h][:, 0, :], ACT.Sigmoid, scale=-1.0)
-            nc.scalar.activation(sig[:, h * HALF : (h + 1) * HALF], scores[h][:, 0, :], ACT.Sigmoid)
+            nc.scalar.activation(sig[:, :, part[h]], dealt(scores[h][:, 0, :]), ACT.Sigmoid)
         a_sum, ta_sum = sums[:, 0, :], sums[:, 1, :]
+        ts = sb.tile([P, SPANS], F32, name="ts")
+        nc.scalar.activation(ts[:], ta_sum, ACT.Copy, scale=1.0 / SPAN)
         neg_s = sb.tile([P, SPANS], F32, name="neg_s")
         neg_max = sb.tile([P, 1], F32, name="neg_max")
         nc.vector.tensor_scalar(neg_s[:], a_sum, -1.0 / SPAN, None, ALU.mult, ALU.min, accum_out=neg_max[:])
         p = sb.tile([P, SPANS], F32, name="p")
         p_sum = sb.tile([P, 1], F32, name="p_sum")
         nc.scalar.activation(p[:], neg_s[:], ACT.Exp, bias=neg_max[:], scale=-1.0, accum_out=p_sum[:])
-        x = sb.tile([P, SLOTS], F32, name="x")
+        x = sb.tile([P, PACK, P], F32, name="x")
         for h in range(HALVES):
-            nc.vector.tensor_tensor(x[:, h * HALF : (h + 1) * HALF], scores[h][:, 1, :], nsig[:, h * HALF : (h + 1) * HALF], ALU.mult)
+            nc.vector.scalar_tensor_tensor(x[:, :, part[h]], sig[:, :, part[h]], 1.0, dealt(scores[h][:, 1, :]), ALU.subtract, ALU.mult)
 
-        def gather_values(b):
+        def gather_values(b, woven):
             got = sb.tile([P, SLOTS], BF16, name=f"got_vals{b}")
             nc.vector.tensor_copy(got[:], pools[b][:].indirect(offsets[:]))
             pairs = got[:].bitcast(F32)
             turned = ps_v.tile([P, 2, P], F32, name="turned")
             for u in range(2):
                 nc.tensor.transpose(turned[:, u, :], pairs[:, u : SLOTS // 2 : 2], identity[:])
-            woven = sb.tile([P, P * PACK], BF16, name=f"woven{b}", align_bytes=64)
-            nc.scalar.copy(woven[:].bitcast(F32).rearrange("p (e u) -> p e u", u=2), turned[:].rearrange("p u e -> p e u"))
-            return woven
+            nc.scalar.copy(woven.bitcast(F32).rearrange("p (e u) -> p e u", u=2), turned[:].rearrange("p u e -> p e u"))
 
-        woven = [gather_values(0)]
+        woven01 = sb.tile([P, 2 * P * PACK], BF16, name="woven01", align_bytes=64)
+        woven2 = sb.tile([P, P * PACK], BF16, name="woven2", align_bytes=64)
+        woven3 = sb.tile([P, P * PACK], BF16, name="woven3", align_bytes=64)
+        gather_values(0, woven01[:, 0 : P * PACK])
         work = in_slot("slot_q", [P, SLOTS + SPANS + 16], F32, "work")
         y, tp = work[:, 0:SLOTS], work[:, SLOTS : SLOTS + SPANS]
         inv_sum, tp_sum = work[:, SLOTS + SPANS : SLOTS + SPANS + 1], work[:, SLOTS + SPANS + 8 : SLOTS + SPANS + 9]
-        nc.vector.scalar_tensor_tensor(
-            y.rearrange("p (g s) -> p g s", s=SPAN), ta_sum.unsqueeze(2).to_broadcast([P, SPANS, SPAN]), 1.0 / SPAN,
-            x[:].rearrange("p (g s) -> p g s", s=SPAN), ALU.mult, ALU.add,
+        nc.vector.tensor_tensor(
+            y.rearrange("p (t g h) -> p t g h", t=PACK, h=2), ts[:].unsqueeze(1).unsqueeze(3).to_broadcast([P, PACK, SPANS, 2]),
+            x[:].rearrange("p t (g h) -> p t g h", h=2), ALU.subtract,
         )
         nc.vector.reciprocal(inv_sum, p_sum[:])
-        nc.vector.scalar_tensor_tensor(tp, p[:], 1.0 / SPAN, ta_sum, ALU.mult, ALU.mult, accum_out=tp_sum)
+        nc.vector.scalar_tensor_tensor(tp, p[:], 1.0, ts[:], ALU.mult, ALU.mult, accum_out=tp_sum)
         mean = sb.tile([P, 1], F32, name="mean")
         nc.scalar.activation(mean[:], tp_sum, ACT.Copy, scale=inv_sum)
         share = sb.tile([P, SPANS, 2], F32, name="share")
         nc.scalar.activation(share[:], p[:].unsqueeze(2).to_broadcast([P, SPANS, 2]), ACT.Copy, scale=inv_sum)
-        woven.append(gather_values(1))
+        gather_values(1, woven01[:, P * PACK : 2 * P * PACK])
         z = in_slot("slot_dq", [P, SLOTS], F32, "z")
-        nc.vector.scalar_tensor_tensor(z[:], y, mean[:], sig[:], ALU.subtract, ALU.mult)
+        nc.vector.scalar_tensor_tensor(z[:], y, mean[:], sig[:].rearrange("p t m -> p (t m)"), ALU.subtract, ALU.mult)
 
         share_t = ps.tile([P, Q], F32, name="share_t")
         nc.tensor.transpose(share_t[:], share[:].rearrange("p g h -> p (g h)"), identity[:])
@@ -148,27 +154,30 @@ def tile_attend_ttspanread_kernel(tc, query, dquery, keys_words, keys_scales, sl
             nc.scalar.activation(weight[:, t, :], share_t[:], ACT.Copy, scale=factor[:, t : t + 1])
         z_t = ps.tile([P, PACK, Q], F32, name="z_t")
         for t in range(PACK):
-            nc.tensor.transpose(z_t[:, t, :], z[:, t:SLOTS:PACK], identity[:])
-        woven.append(gather_values(2))
+            nc.tensor.transpose(z_t[:, t, :], z[:, t * P : (t + 1) * P], identity[:])
+        gather_values(2, woven2[:])
         w_bf = in_slot("dq_bf", [P, Q, PACK], BF16, "w_bf")
-        nc.vector.tensor_tensor(w_bf[:], z_t[:].rearrange("p t q -> p q t"), weight[:].rearrange("p t q -> p q t"), ALU.mult)
-        w_codes = sb.tile([P, Q], U32, name="w_codes", align_bytes=64)
-        w_scales = sb.tile([P, Q], U8, name="w_scales", align_bytes=64)
-        nc.vector.quantize_mx(out=w_codes[:].bitcast(FP8X4), scales=w_scales[:], in_=w_bf[:].rearrange("p q t -> p (q t)"))
-        woven.append(gather_values(3))
+        nc.vector.tensor_tensor(
+            w_bf[:].rearrange("p (c i) t -> p c t i", i=LINE), z_t[:].rearrange("p t (c i) -> p c t i", i=LINE),
+            weight[:].rearrange("p t (c i) -> p c t i", i=LINE), ALU.mult,
+        )
+        gather_values(3, woven3[:])
 
-        v_codes = in_slot("slot_k", [P, E - P], U32, "v_codes")
+        late_codes = in_slot("slot_k", [P, E], U32, "late_codes")
+        w_codes, v_codes = late_codes[:, 0:Q], late_codes[:, Q:E]
+        w_scales = sb.tile([P, Q], U8, name="w_scales", align_bytes=64)
         v_scales = sb.tile([P, E - P], U8, name="v_scales", align_bytes=64)
         v_codes_last = sb.tile([P, P], U32, name="v_codes_last", align_bytes=64)
         v_scales_last = sb.tile([P, P], U8, name="v_scales_last", align_bytes=64)
-        for b in range(BLOCKS - 1):
-            nc.vector.quantize_mx(out=v_codes[:, b * P : (b + 1) * P].bitcast(FP8X4), scales=v_scales[:, b * P : (b + 1) * P], in_=woven[b][:])
-        nc.vector.quantize_mx(out=v_codes_last[:].bitcast(FP8X4), scales=v_scales_last[:], in_=woven[BLOCKS - 1][:])
+        nc.vector.quantize_mx(out=w_codes.bitcast(FP8X4), scales=w_scales[:], in_=w_bf[:].rearrange("p q t -> p (q t)"))
+        nc.vector.quantize_mx(out=v_codes[:, 0 : 2 * P].bitcast(FP8X4), scales=v_scales[:, 0 : 2 * P], in_=woven01[:])
+        nc.vector.quantize_mx(out=v_codes[:, 2 * P : 3 * P].bitcast(FP8X4), scales=v_scales[:, 2 * P : 3 * P], in_=woven2[:])
+        nc.vector.quantize_mx(out=v_codes_last[:].bitcast(FP8X4), scales=v_scales_last[:], in_=woven3[:])
 
-        def product(bank, codes, scales):
+        def product(bank, rhs_codes, rhs_scales):
             nc.tensor.matmul_mx(
-                out=bank, lhsT=w_codes[:].bitcast(FP8X4), lhsT_scale=w_scales[:],
-                rhs=codes.bitcast(FP8X4), rhs_scale=scales, start=True, stop=True,
+                out=bank, lhsT=w_codes.bitcast(FP8X4), lhsT_scale=w_scales[:],
+                rhs=rhs_codes.bitcast(FP8X4), rhs_scale=rhs_scales, start=True, stop=True,
             )
 
         o_first = ps.tile([P, E - P], F32, name="o_first")

@@ -20,10 +20,14 @@ AXIS = mybir.AxisListType
 
 P = 128
 PACK = 4
-BLOCKS = E // P
+QUADRANT = 32
+SCALE_ROWS = D // 32
+PER_COLUMN = 16
 HALVES = 2
 HALF = SLOTS // HALVES
+SPAN_PARTS = SPAN // PACK
 LINE = 4
+PAIR = 2 * P
 
 
 def tile_attend_ttspanread_kernel(tc, query, dquery, keys_words, keys_scales, slot_factor, vals, offs, out):
@@ -31,12 +35,23 @@ def tile_attend_ttspanread_kernel(tc, query, dquery, keys_words, keys_scales, sl
     with ExitStack() as ctx:
         sb = ctx.enter_context(tc.tile_pool(name="sb", bufs=1))
         ps = ctx.enter_context(tc.psum_pool(name="ps", bufs=1))
-        ps_v = ctx.enter_context(tc.psum_pool(name="ps_v", bufs=2))
 
         def in_slot(slot, shape, dtype, name):
             return sb.tile(shape, dtype, name=name, tag=slot, align_bytes=64)
 
-        offsets = sb.tile([P, SLOTS // 16], U16, name="offsets")
+        def aligned(shape, dtype, name):
+            return sb.tile(shape, dtype, name=name, align_bytes=64)
+
+        def quantize(codes, scales, rounded):
+            nc.vector.quantize_mx(out=codes.bitcast(FP8X4), scales=scales, in_=rounded)
+
+        def multiply(bank, lhs_codes, lhs_scales, rhs_codes, rhs_scales):
+            nc.tensor.matmul_mx(
+                out=bank, lhsT=lhs_codes.bitcast(FP8X4), lhsT_scale=lhs_scales,
+                rhs=rhs_codes.bitcast(FP8X4), rhs_scale=rhs_scales, start=True, stop=True,
+            )
+
+        offsets = sb.tile([P, SLOTS // PER_COLUMN], U16, name="offsets")
         key_bytes = sb.tile([P, T], U8, name="key_bytes")
         nc.gpsimd.memset(key_bytes[:].bitcast(I32), 0)
         identity = sb.tile([P, P], F32, name="identity")
@@ -44,151 +59,160 @@ def tile_attend_ttspanread_kernel(tc, query, dquery, keys_words, keys_scales, sl
 
         q_raw = in_slot("slot_q", [P, PACK, Q], F32, "q_raw")
         dq_raw = in_slot("slot_dq", [P, PACK, Q], F32, "dq_raw")
-        key_words = in_slot("slot_k", [P, T], U32, "key_words")
+        key_words = in_slot("slot_keys", [P, T], U32, "key_words")
         nc.sync.dma_start(offsets[:], offs)
         nc.sync.dma_start(q_raw[:], query.rearrange("(p j) q -> p j q", j=PACK))
         nc.sync.dma_start(dq_raw[:], dquery.rearrange("(p j) q -> p j q", j=PACK))
-        for quad in range(4):
-            nc.sync.dma_start(
-                key_bytes[32 * quad : 32 * quad + 4, :].bitcast(I32),
-                keys_scales[0, 4 * quad : 4 * quad + 4, :].bitcast(I32),
-            )
+        for r in range(PACK):
+            nc.sync.dma_start(key_bytes[r:P:QUADRANT, :].bitcast(I32), keys_scales[0, r:SCALE_ROWS:PACK, :].bitcast(I32))
         nc.sync.dma_start(key_words[:].bitcast(I32), keys_words[0].rearrange("p n t -> p (n t)").bitcast(I32))
-        pools = {}
 
-        def load_values(b, slot):
-            pools[b] = in_slot(slot, [P, T], F32, f"vals{b}")
-            nc.sync.dma_start(pools[b][:], vals[b * P : (b + 1) * P, :])
+        def load_values(block, slot):
+            pool = in_slot(slot, [P, T], F32, f"vals{block}")
+            nc.sync.dma_start(pool[:], vals[block * P : (block + 1) * P, :])
+            return pool
 
         def quantize_rows(raw, name, round_rows):
-            rounded = in_slot(name + "_bf", [P, Q, PACK], BF16, name + "_bf")
+            rounded = in_slot("slot_" + name + "_rounded", [P, Q, PACK], BF16, name + "_rounded")
             round_rows(rounded[:].rearrange("p (c i) j -> p c j i", i=LINE), raw[:].rearrange("p j (c i) -> p c j i", i=LINE))
-            codes = sb.tile([P, Q], U32, name=name + "_codes", align_bytes=64)
-            scales = sb.tile([P, Q], U8, name=name + "_scales", align_bytes=64)
-            nc.vector.quantize_mx(out=codes[:].bitcast(FP8X4), scales=scales[:], in_=rounded[:].rearrange("p q j -> p (q j)"))
+            codes = aligned([P, Q], U32, name + "_codes")
+            scales = aligned([P, Q], U8, name + "_scales")
+            quantize(codes[:], scales[:], rounded[:].rearrange("p q j -> p (q j)"))
             return codes, scales
 
-        got_bytes = sb.tile([P, SLOTS], U8, name="got_bytes", align_bytes=64)
+        got_bytes = aligned([P, SLOTS], U8, "got_bytes")
+        nc.vector.tensor_copy(got_bytes[:], key_bytes[:].indirect(offsets[:]))
         q_mx = quantize_rows(q_raw, "q", nc.vector.tensor_copy)
-        load_values(0, "slot_q")
+        vals2 = load_values(2, "slot_q")
         dq_mx = quantize_rows(dq_raw, "dq", lambda dst, src: nc.scalar.activation(dst, src, ACT.Copy))
-        load_values(1, "slot_dq")
-        load_values(2, "dq_bf")
-        factor = in_slot("q_bf", [P, PACK], F32, "factor")
+        vals0 = load_values(0, "slot_dq")
+        vals1 = load_values(1, "slot_dq_rounded")
+        factor = in_slot("slot_q_rounded", [P, PACK], F32, "factor")
         nc.sync.dma_start(factor[:], slot_factor.rearrange("o (p t) -> p (o t)", t=PACK))
 
-        got_words = sb.tile([P, SLOTS], U32, name="got_words", align_bytes=64)
-        nc.vector.tensor_copy(got_words[:], key_words[:].indirect(offsets[:]))
+        got_words = aligned([P, SLOTS], U32, "got_words")
         scores = []
         for h in range(HALVES):
             cols = slice(h * HALF, (h + 1) * HALF)
-            nc.vector.tensor_copy(got_bytes[:, cols], key_bytes[:].indirect(offsets[:, h * HALF // 16 : (h + 1) * HALF // 16]))
-            bank = ps.tile([P, 2, HALF], F32, name=f"scores{h}")
-            for c, (codes, scales) in enumerate((q_mx, dq_mx)):
-                nc.tensor.matmul_mx(
-                    out=bank[:, c, :], lhsT=codes[:].bitcast(FP8X4), lhsT_scale=scales[:],
-                    rhs=got_words[:, cols].bitcast(FP8X4), rhs_scale=got_bytes[:, cols], start=True, stop=True,
-                )
+            entries = offsets[:, h * HALF // PER_COLUMN : (h + 1) * HALF // PER_COLUMN]
+            nc.vector.tensor_copy(got_words[:, cols], key_words[:].indirect(entries))
+            bank = ps.tile([P, 2, HALF], F32, name=f"scores{h}", tag=f"scores{h}")
+            for plane, (codes, scales) in enumerate((q_mx, dq_mx)):
+                multiply(bank[:, plane, :], codes[:], scales[:], got_words[:, cols], got_bytes[:, cols])
             scores.append(bank)
-        load_values(3, "slot_k")
+        vals3 = load_values(3, "slot_keys")
 
-        def dealt(scores_half):
-            return scores_half.rearrange("p (m t) -> p t m", t=PACK)
+        def dealt(half_plane):
+            return half_plane.rearrange("p (m t) -> p t m", t=PACK)
 
         sums = sb.tile([P, 2, SPANS], F32, name="sums")
         sig = sb.tile([P, PACK, P], F32, name="sig")
-        part = [slice(h * P // HALVES, (h + 1) * P // HALVES) for h in range(HALVES)]
+        dealt_half = [slice(h * P // HALVES, (h + 1) * P // HALVES) for h in range(HALVES)]
         for h in range(HALVES):
             nc.vector.tensor_reduce(
                 sums[:, :, h * SPANS // HALVES : (h + 1) * SPANS // HALVES],
                 scores[h][:].rearrange("p c (g s) -> p c g s", s=SPAN), AXIS.X, ALU.add,
             )
-            nc.scalar.activation(sig[:, :, part[h]], dealt(scores[h][:, 0, :]), ACT.Sigmoid)
-        a_sum, ta_sum = sums[:, 0, :], sums[:, 1, :]
-        ts = sb.tile([P, SPANS], F32, name="ts")
-        nc.scalar.activation(ts[:], ta_sum, ACT.Copy, scale=1.0 / SPAN)
-        neg_s = sb.tile([P, SPANS], F32, name="neg_s")
+            nc.scalar.activation(sig[:, :, dealt_half[h]], dealt(scores[h][:, 0, :]), ACT.Sigmoid)
+
+        neg_s = in_slot("slot_scalar", [P, SPANS], F32, "neg_s")
         neg_max = sb.tile([P, 1], F32, name="neg_max")
-        nc.vector.tensor_scalar(neg_s[:], a_sum, -1.0 / SPAN, None, ALU.mult, ALU.min, accum_out=neg_max[:])
+        nc.vector.tensor_scalar(neg_s[:], sums[:, 0, :], -1.0 / SPAN, None, ALU.mult, ALU.min, accum_out=neg_max[:])
+        ts = sb.tile([P, SPANS], F32, name="ts")
+        nc.vector.tensor_scalar(ts[:], sums[:, 1, :], 1.0 / SPAN, None, ALU.mult)
         p = sb.tile([P, SPANS], F32, name="p")
         p_sum = sb.tile([P, 1], F32, name="p_sum")
         nc.scalar.activation(p[:], neg_s[:], ACT.Exp, bias=neg_max[:], scale=-1.0, accum_out=p_sum[:])
-        x = sb.tile([P, PACK, P], F32, name="x")
-        for h in range(HALVES):
-            nc.vector.scalar_tensor_tensor(x[:, :, part[h]], sig[:, :, part[h]], 1.0, dealt(scores[h][:, 1, :]), ALU.subtract, ALU.mult)
 
-        def gather_values(b, woven):
-            got = sb.tile([P, SLOTS], BF16, name=f"got_vals{b}")
-            nc.vector.tensor_copy(got[:], pools[b][:].indirect(offsets[:]))
+        neg_own = in_slot("slot_own", [P, PACK, P], F32, "neg_own")
+        for h in range(HALVES):
+            nc.vector.scalar_tensor_tensor(
+                neg_own[:, :, dealt_half[h]], sig[:, :, dealt_half[h]], 1.0, dealt(scores[h][:, 1, :]), ALU.subtract, ALU.mult
+            )
+        change = sb.tile([P, SLOTS], F32, name="change")
+        nc.vector.tensor_tensor(
+            change[:].rearrange("p (t g h) -> p t g h", t=PACK, h=SPAN_PARTS),
+            ts[:].unsqueeze(1).unsqueeze(3).to_broadcast([P, PACK, SPANS, SPAN_PARTS]),
+            neg_own[:].rearrange("p t (g h) -> p t g h", h=SPAN_PARTS), ALU.subtract,
+        )
+
+        def turn(got, bank_tag):
             pairs = got[:].bitcast(F32)
-            turned = ps_v.tile([P, 2, P], F32, name="turned")
+            turned = ps.tile([P, 2, P], F32, name="turned", tag=bank_tag)
             for u in range(2):
                 nc.tensor.transpose(turned[:, u, :], pairs[:, u : SLOTS // 2 : 2], identity[:])
+            return turned
+
+        def weave(turned, woven):
             nc.scalar.copy(woven.bitcast(F32).rearrange("p (e u) -> p e u", u=2), turned[:].rearrange("p u e -> p e u"))
 
-        woven01 = sb.tile([P, 2 * P * PACK], BF16, name="woven01", align_bytes=64)
-        woven2 = sb.tile([P, P * PACK], BF16, name="woven2", align_bytes=64)
-        woven3 = sb.tile([P, P * PACK], BF16, name="woven3", align_bytes=64)
-        gather_values(0, woven01[:, 0 : P * PACK])
-        work = in_slot("slot_q", [P, SLOTS + SPANS + 16], F32, "work")
-        y, tp = work[:, 0:SLOTS], work[:, SLOTS : SLOTS + SPANS]
+        def gather_values(pool, slot, bank_tag):
+            got = in_slot(slot, [P, SLOTS], BF16, "got_" + bank_tag)
+            nc.vector.tensor_copy(got[:], pool[:].indirect(offsets[:]))
+            return turn(got, bank_tag)
+
+        turned0 = gather_values(vals0, "slot_own", "turned0")
+
+        work = in_slot("slot_dq", [P, SLOTS + SPANS + 16], F32, "work")
+        unshared, tp = work[:, 0:SLOTS], work[:, SLOTS : SLOTS + SPANS]
         inv_sum, tp_sum = work[:, SLOTS + SPANS : SLOTS + SPANS + 1], work[:, SLOTS + SPANS + 8 : SLOTS + SPANS + 9]
-        nc.vector.tensor_tensor(
-            y.rearrange("p (t g h) -> p t g h", t=PACK, h=2), ts[:].unsqueeze(1).unsqueeze(3).to_broadcast([P, PACK, SPANS, 2]),
-            x[:].rearrange("p t (g h) -> p t g h", h=2), ALU.subtract,
-        )
         nc.vector.reciprocal(inv_sum, p_sum[:])
         nc.vector.scalar_tensor_tensor(tp, p[:], 1.0, ts[:], ALU.mult, ALU.mult, accum_out=tp_sum)
+        share = sb.tile([P, SPANS, SPAN_PARTS], F32, name="share")
+        nc.vector.tensor_scalar(share[:], p[:].unsqueeze(2).to_broadcast([P, SPANS, SPAN_PARTS]), inv_sum, None, ALU.mult)
         mean = sb.tile([P, 1], F32, name="mean")
-        nc.scalar.activation(mean[:], tp_sum, ACT.Copy, scale=inv_sum)
-        share = sb.tile([P, SPANS, 2], F32, name="share")
-        nc.scalar.activation(share[:], p[:].unsqueeze(2).to_broadcast([P, SPANS, 2]), ACT.Copy, scale=inv_sum)
-        gather_values(1, woven01[:, P * PACK : 2 * P * PACK])
-        z = in_slot("slot_dq", [P, SLOTS], F32, "z")
-        nc.vector.scalar_tensor_tensor(z[:], y, mean[:], sig[:].rearrange("p t m -> p (t m)"), ALU.subtract, ALU.mult)
+        nc.vector.tensor_scalar(mean[:], tp_sum, inv_sum, None, ALU.mult)
+        nc.vector.scalar_tensor_tensor(unshared, change[:], mean[:], sig[:].rearrange("p t m -> p (t m)"), ALU.subtract, ALU.mult)
 
-        share_t = ps.tile([P, Q], F32, name="share_t")
+        share_t = ps.tile([P, Q], F32, name="share_t", tag="scores0")
         nc.tensor.transpose(share_t[:], share[:].rearrange("p g h -> p (g h)"), identity[:])
-        weight = sb.tile([P, PACK, Q], F32, name="weight")
+        unshared_t = ps.tile([P, PACK, Q], F32, name="unshared_t")
         for t in range(PACK):
-            nc.scalar.activation(weight[:, t, :], share_t[:], ACT.Copy, scale=factor[:, t : t + 1])
-        z_t = ps.tile([P, PACK, Q], F32, name="z_t")
+            nc.tensor.transpose(unshared_t[:, t, :], unshared[:, t * P : (t + 1) * P], identity[:])
+        turned1 = gather_values(vals1, "slot_got1", "turned1")
+
+        rounded2 = in_slot("slot_scalar", [P, T], BF16, "rounded2")
+        nc.scalar.activation(rounded2[:], vals2[:], ACT.Copy)
+        got2 = in_slot("slot_got2", [P, SLOTS], BF16, "got2")
+        nc.scalar.activation(got2[:], rounded2[:].indirect(offsets[:]), ACT.Copy)
+        turned2 = turn(got2, "turned23")
+        share_factor = in_slot("slot_scalar", [P, PACK, Q], F32, "share_factor")
         for t in range(PACK):
-            nc.tensor.transpose(z_t[:, t, :], z[:, t * P : (t + 1) * P], identity[:])
-        gather_values(2, woven2[:])
-        w_bf = in_slot("dq_bf", [P, Q, PACK], BF16, "w_bf")
+            nc.scalar.activation(share_factor[:, t, :], share_t[:], ACT.Copy, scale=factor[:, t : t + 1])
+        woven2 = aligned([P, P * PACK], BF16, "woven2")
+        weave(turned2, woven2[:])
+        woven01 = in_slot("slot_got2", [P, PAIR * PACK], BF16, "woven01")
+        weave(turned0, woven01[:, 0 : P * PACK])
+        weave(turned1, woven01[:, P * PACK : PAIR * PACK])
+        turned3 = gather_values(vals3, "slot_got3", "turned23")
+        woven3 = aligned([P, P * PACK], BF16, "woven3")
+        weave(turned3, woven3[:])
+
+        w_rounded = in_slot("slot_keys", [P, Q, PACK], BF16, "w_rounded")
         nc.vector.tensor_tensor(
-            w_bf[:].rearrange("p (c i) t -> p c t i", i=LINE), z_t[:].rearrange("p t (c i) -> p c t i", i=LINE),
-            weight[:].rearrange("p t (c i) -> p c t i", i=LINE), ALU.mult,
+            w_rounded[:].rearrange("p (c i) t -> p c t i", i=LINE),
+            unshared_t[:].rearrange("p t (c i) -> p c t i", i=LINE),
+            share_factor[:].rearrange("p t (c i) -> p c t i", i=LINE), ALU.mult,
         )
-        gather_values(3, woven3[:])
+        v_codes = in_slot("slot_scalar", [P, E - P], U32, "v_codes")
+        v_scales = aligned([P, E - P], U8, "v_scales")
+        v3_codes = aligned([P, P], U32, "v3_codes")
+        v3_scales = aligned([P, P], U8, "v3_scales")
+        w_codes = aligned([P, Q], U32, "w_codes")
+        w_scales = aligned([P, Q], U8, "w_scales")
+        quantize(v_codes[:, PAIR : E - P], v_scales[:, PAIR : E - P], woven2[:])
+        quantize(w_codes[:], w_scales[:], w_rounded[:].rearrange("p q t -> p (q t)"))
+        quantize(v_codes[:, 0:PAIR], v_scales[:, 0:PAIR], woven01[:])
+        quantize(v3_codes[:], v3_scales[:], woven3[:])
 
-        late_codes = in_slot("slot_k", [P, E], U32, "late_codes")
-        w_codes, v_codes = late_codes[:, 0:Q], late_codes[:, Q:E]
-        w_scales = sb.tile([P, Q], U8, name="w_scales", align_bytes=64)
-        v_scales = sb.tile([P, E - P], U8, name="v_scales", align_bytes=64)
-        v_codes_last = sb.tile([P, P], U32, name="v_codes_last", align_bytes=64)
-        v_scales_last = sb.tile([P, P], U8, name="v_scales_last", align_bytes=64)
-        nc.vector.quantize_mx(out=w_codes.bitcast(FP8X4), scales=w_scales[:], in_=w_bf[:].rearrange("p q t -> p (q t)"))
-        nc.vector.quantize_mx(out=v_codes[:, 0 : 2 * P].bitcast(FP8X4), scales=v_scales[:, 0 : 2 * P], in_=woven01[:])
-        nc.vector.quantize_mx(out=v_codes[:, 2 * P : 3 * P].bitcast(FP8X4), scales=v_scales[:, 2 * P : 3 * P], in_=woven2[:])
-        nc.vector.quantize_mx(out=v_codes_last[:].bitcast(FP8X4), scales=v_scales_last[:], in_=woven3[:])
-
-        def product(bank, rhs_codes, rhs_scales):
-            nc.tensor.matmul_mx(
-                out=bank, lhsT=w_codes.bitcast(FP8X4), lhsT_scale=w_scales[:],
-                rhs=rhs_codes.bitcast(FP8X4), rhs_scale=rhs_scales, start=True, stop=True,
-            )
-
-        o_first = ps.tile([P, E - P], F32, name="o_first")
-        product(o_first[:, 0 : 2 * P], v_codes[:, 0 : 2 * P], v_scales[:, 0 : 2 * P])
-        product(o_first[:, 2 * P : 3 * P], v_codes[:, 2 * P : 3 * P], v_scales[:, 2 * P : 3 * P])
-        res_first = sb.tile([P, E - P], F32, name="res_first")
-        nc.scalar.copy(res_first[:], o_first[:])
-        nc.sync.dma_start(out[:, 0 : E - P], res_first[:])
-
-        o_last = ps.tile([P, P], F32, name="o_last")
-        product(o_last[:], v_codes_last[:], v_scales_last[:])
-        res_last = sb.tile([P, P], F32, name="res_last")
-        nc.vector.tensor_copy(res_last[:], o_last[:])
-        nc.sync.dma_start(out[:, E - P : E], res_last[:])
+        low = ps.tile([P, PAIR], F32, name="low", tag="scores1")
+        high = ps.tile([P, PAIR], F32, name="high")
+        multiply(high[:, 0:P], w_codes[:], w_scales[:], v_codes[:, PAIR : E - P], v_scales[:, PAIR : E - P])
+        multiply(low[:], w_codes[:], w_scales[:], v_codes[:, 0:PAIR], v_scales[:, 0:PAIR])
+        multiply(high[:, P:PAIR], w_codes[:], w_scales[:], v3_codes[:], v3_scales[:])
+        out_low = sb.tile([P, PAIR], F32, name="out_low")
+        nc.scalar.copy(out_low[:], low[:])
+        nc.sync.dma_start(out[:, 0:PAIR], out_low[:])
+        out_high = sb.tile([P, PAIR], F32, name="out_high")
+        nc.vector.tensor_copy(out_high[:], high[:])
+        nc.sync.dma_start(out[:, PAIR:E], out_high[:])

@@ -27,6 +27,7 @@ HALVES = 2
 HALF = SLOTS // HALVES
 SPAN_PARTS = SPAN // PACK
 LINE = 4
+BLOCK32 = 8
 PAIR = 2 * P
 
 
@@ -105,7 +106,7 @@ def tile_attend_ttspanread_kernel(tc, query, dquery, keys_words, keys_scales, sl
         def dealt(half_plane):
             return half_plane.rearrange("p (m t) -> p t m", t=PACK)
 
-        sums = sb.tile([P, 2, SPANS], F32, name="sums")
+        sums = in_slot("slot_sums", [P, 2, SPANS], F32, "sums")
         sig = sb.tile([P, PACK, P], F32, name="sig")
         dealt_half = [slice(h * P // HALVES, (h + 1) * P // HALVES) for h in range(HALVES)]
         for h in range(HALVES):
@@ -115,26 +116,20 @@ def tile_attend_ttspanread_kernel(tc, query, dquery, keys_words, keys_scales, sl
             )
             nc.scalar.activation(sig[:, :, dealt_half[h]], dealt(scores[h][:, 0, :]), ACT.Sigmoid)
 
-        neg_s = in_slot("slot_scalar", [P, SPANS], F32, "neg_s")
-        neg_max = sb.tile([P, 1], F32, name="neg_max")
-        nc.vector.tensor_scalar(neg_s[:], sums[:, 0, :], -1.0 / SPAN, None, ALU.mult, ALU.min, accum_out=neg_max[:])
-        ts = sb.tile([P, SPANS], F32, name="ts")
-        nc.vector.tensor_scalar(ts[:], sums[:, 1, :], 1.0 / SPAN, None, ALU.mult)
+        means = sb.tile([P, 2, SPANS], F32, name="means")
+        nc.vector.tensor_scalar(means[:], sums[:], 1.0 / SPAN, None, ALU.mult)
+        s_mean, ts = means[:, 0, :], means[:, 1, :]
+        neg_max = in_slot("slot_scalar", [P, 1], F32, "neg_max")
+        nc.vector.tensor_reduce(neg_max[:], s_mean, AXIS.X, ALU.max, negate=True)
         p = sb.tile([P, SPANS], F32, name="p")
         p_sum = sb.tile([P, 1], F32, name="p_sum")
-        nc.scalar.activation(p[:], neg_s[:], ACT.Exp, bias=neg_max[:], scale=-1.0, accum_out=p_sum[:])
+        nc.scalar.activation(p[:], s_mean, ACT.Exp, bias=neg_max[:], accum_out=p_sum[:])
 
-        neg_own = in_slot("slot_own", [P, PACK, P], F32, "neg_own")
+        neg_own = sb.tile([P, PACK, P], F32, name="neg_own")
         for h in range(HALVES):
             nc.vector.scalar_tensor_tensor(
                 neg_own[:, :, dealt_half[h]], sig[:, :, dealt_half[h]], 1.0, dealt(scores[h][:, 1, :]), ALU.subtract, ALU.mult
             )
-        change = sb.tile([P, SLOTS], F32, name="change")
-        nc.vector.tensor_tensor(
-            change[:].rearrange("p (t g h) -> p t g h", t=PACK, h=SPAN_PARTS),
-            ts[:].unsqueeze(1).unsqueeze(3).to_broadcast([P, PACK, SPANS, SPAN_PARTS]),
-            neg_own[:].rearrange("p t (g h) -> p t g h", h=SPAN_PARTS), ALU.subtract,
-        )
 
         def turn(got, bank_tag):
             pairs = got[:].bitcast(F32)
@@ -151,24 +146,35 @@ def tile_attend_ttspanread_kernel(tc, query, dquery, keys_words, keys_scales, sl
             nc.vector.tensor_copy(got[:], pool[:].indirect(offsets[:]))
             return turn(got, bank_tag)
 
-        turned0 = gather_values(vals0, "slot_own", "turned0")
+        turned0 = gather_values(vals0, "slot_sums", "turned0")
 
-        work = in_slot("slot_dq", [P, SLOTS + SPANS + 16], F32, "work")
-        unshared, tp = work[:, 0:SLOTS], work[:, SLOTS : SLOTS + SPANS]
-        inv_sum, tp_sum = work[:, SLOTS + SPANS : SLOTS + SPANS + 1], work[:, SLOTS + SPANS + 8 : SLOTS + SPANS + 9]
+        rows = in_slot("slot_dq", [P, SPANS + 2 * BLOCK32], F32, "rows")
+        tp, inv_sum, tp_sum = rows[:, 0:SPANS], rows[:, SPANS : SPANS + 1], rows[:, SPANS + BLOCK32 : SPANS + BLOCK32 + 1]
         nc.vector.reciprocal(inv_sum, p_sum[:])
-        nc.vector.scalar_tensor_tensor(tp, p[:], 1.0, ts[:], ALU.mult, ALU.mult, accum_out=tp_sum)
-        share = sb.tile([P, SPANS, SPAN_PARTS], F32, name="share")
-        nc.vector.tensor_scalar(share[:], p[:].unsqueeze(2).to_broadcast([P, SPANS, SPAN_PARTS]), inv_sum, None, ALU.mult)
-        mean = sb.tile([P, 1], F32, name="mean")
-        nc.vector.tensor_scalar(mean[:], tp_sum, inv_sum, None, ALU.mult)
-        nc.vector.scalar_tensor_tensor(unshared, change[:], mean[:], sig[:].rearrange("p t m -> p (t m)"), ALU.subtract, ALU.mult)
+        nc.vector.scalar_tensor_tensor(tp, p[:], 1.0, ts, ALU.mult, ALU.mult, accum_out=tp_sum)
 
-        share_t = ps.tile([P, Q], F32, name="share_t", tag="scores0")
-        nc.tensor.transpose(share_t[:], share[:].rearrange("p g h -> p (g h)"), identity[:])
-        unshared_t = ps.tile([P, PACK, Q], F32, name="unshared_t")
+        shares = in_slot("slot_shares", [P, P + BLOCK32], F32, "shares")
+        neg_share, mean = shares[:, 0:P], shares[:, P : P + 1]
+
+        def by_column(per_span):
+            return per_span.unsqueeze(2).to_broadcast([P, SPANS, SPAN_PARTS])
+
+        nc.vector.tensor_scalar(neg_share.rearrange("p (g h) -> p g h", h=SPAN_PARTS), by_column(p[:]), inv_sum, -1.0, ALU.mult, ALU.mult)
+        nc.vector.tensor_scalar(mean, tp_sum, inv_sum, None, ALU.mult)
+        neg_gate = sb.tile([P, PACK, P], F32, name="neg_gate")
+        nc.vector.tensor_tensor(neg_gate[:], sig[:], neg_share.unsqueeze(1).to_broadcast([P, PACK, P]), ALU.mult)
+        neg_span = sb.tile([P, SPANS, SPAN_PARTS], F32, name="neg_span")
+        nc.vector.tensor_scalar(neg_span[:], by_column(ts), mean, -1.0, ALU.subtract, ALU.mult)
+
+        neg_gate_t = ps.tile([P, PACK, Q], F32, name="neg_gate_t", tag="scores0")
+        neg_bracket_t = ps.tile([P, PACK, Q], F32, name="neg_bracket_t")
         for t in range(PACK):
-            nc.tensor.transpose(unshared_t[:, t, :], unshared[:, t * P : (t + 1) * P], identity[:])
+            nc.tensor.transpose(neg_gate_t[:, t, :], neg_gate[:, t, :], identity[:])
+        for t in range(PACK):
+            nc.tensor.matmul(neg_bracket_t[:, t, :], neg_own[:, t, :], identity[:], start=True, stop=False, is_transpose=True)
+            nc.tensor.matmul(
+                neg_bracket_t[:, t, :], neg_span[:].rearrange("p g h -> p (g h)"), identity[:], start=False, stop=True, is_transpose=True
+            )
         turned1 = gather_values(vals1, "slot_got1", "turned1")
 
         rounded2 = in_slot("slot_scalar", [P, T], BF16, "rounded2")
@@ -176,23 +182,23 @@ def tile_attend_ttspanread_kernel(tc, query, dquery, keys_words, keys_scales, sl
         got2 = in_slot("slot_got2", [P, SLOTS], BF16, "got2")
         nc.scalar.activation(got2[:], rounded2[:].indirect(offsets[:]), ACT.Copy)
         turned2 = turn(got2, "turned23")
-        share_factor = in_slot("slot_scalar", [P, PACK, Q], F32, "share_factor")
+        neg_factor = in_slot("slot_scalar", [P, PACK, Q], F32, "neg_factor")
         for t in range(PACK):
-            nc.scalar.activation(share_factor[:, t, :], share_t[:], ACT.Copy, scale=factor[:, t : t + 1])
+            nc.scalar.activation(neg_factor[:, t, :], neg_gate_t[:, t, :], ACT.Copy, scale=factor[:, t : t + 1])
         woven2 = aligned([P, P * PACK], BF16, "woven2")
         weave(turned2, woven2[:])
         woven01 = in_slot("slot_got2", [P, PAIR * PACK], BF16, "woven01")
         weave(turned0, woven01[:, 0 : P * PACK])
         weave(turned1, woven01[:, P * PACK : PAIR * PACK])
-        turned3 = gather_values(vals3, "slot_got3", "turned23")
+        turned3 = gather_values(vals3, "slot_shares", "turned23")
         woven3 = aligned([P, P * PACK], BF16, "woven3")
         weave(turned3, woven3[:])
 
         w_rounded = in_slot("slot_keys", [P, Q, PACK], BF16, "w_rounded")
         nc.vector.tensor_tensor(
             w_rounded[:].rearrange("p (c i) t -> p c t i", i=LINE),
-            unshared_t[:].rearrange("p t (c i) -> p c t i", i=LINE),
-            share_factor[:].rearrange("p t (c i) -> p c t i", i=LINE), ALU.mult,
+            neg_bracket_t[:].rearrange("p t (c i) -> p c t i", i=LINE),
+            neg_factor[:].rearrange("p t (c i) -> p c t i", i=LINE), ALU.mult,
         )
         v_codes = in_slot("slot_scalar", [P, E - P], U32, "v_codes")
         v_scales = aligned([P, E - P], U8, "v_scales")

from contextlib import ExitStack

import concourse.mybir as mybir
from concourse.masks import make_identity

D, E, T, SLOTS, Q, SPANS = 512, 512, 2048, 512, 128, 64
SPAN = SLOTS // SPANS
FLOPS = 2 * Q * SLOTS * D * 2 + 2 * Q * SLOTS * E

F32 = mybir.dt.float32
BF16 = mybir.dt.bfloat16
I32 = mybir.dt.int32
U32 = mybir.dt.uint32
U16 = mybir.dt.uint16
U8 = mybir.dt.uint8
FP8X4 = mybir.dt.float8_e4m3fn_x4
ALU = mybir.AluOpType
ACT = mybir.ActivationFunctionType
AXIS = mybir.AxisListType

P = 128
PACK = 4
QUADRANT = 32
SCALE_ROWS = D // 32
PER_COLUMN = 16
HALVES = 2
HALF = SLOTS // HALVES
SPAN_PARTS = SPAN // PACK
LINE = 4
BLOCK32 = 8
PAIR = 2 * P


def tile_attend_ttspanread_kernel(tc, query, dquery, keys_words, keys_scales, slot_factor, vals, offs, out):
    nc = tc.nc
    with ExitStack() as ctx:
        sb = ctx.enter_context(tc.tile_pool(name="sb", bufs=1))
        ps = ctx.enter_context(tc.psum_pool(name="ps", bufs=1))

        def in_slot(slot, shape, dtype, name):
            return sb.tile(shape, dtype, name=name, tag=slot, align_bytes=64)

        def aligned(shape, dtype, name):
            return sb.tile(shape, dtype, name=name, align_bytes=64)

        def quantize(codes, scales, rounded):
            nc.vector.quantize_mx(out=codes.bitcast(FP8X4), scales=scales, in_=rounded)

        def multiply(bank, lhs_codes, lhs_scales, rhs_codes, rhs_scales):
            nc.tensor.matmul_mx(
                out=bank, lhsT=lhs_codes.bitcast(FP8X4), lhsT_scale=lhs_scales,
                rhs=rhs_codes.bitcast(FP8X4), rhs_scale=rhs_scales, start=True, stop=True,
            )

        offsets = sb.tile([P, SLOTS // PER_COLUMN], U16, name="offsets")
        key_bytes = sb.tile([P, T], U8, name="key_bytes")
        nc.gpsimd.memset(key_bytes[:].bitcast(I32), 0)
        identity = sb.tile([P, P], F32, name="identity")
        make_identity(nc, identity[:])

        q_raw = in_slot("slot_q", [P, PACK, Q], F32, "q_raw")
        dq_raw = in_slot("slot_dq", [P, PACK, Q], F32, "dq_raw")
        key_words = in_slot("slot_keys", [P, T], U32, "key_words")
        nc.sync.dma_start(offsets[:], offs)
        nc.sync.dma_start(q_raw[:], query.rearrange("(p j) q -> p j q", j=PACK))
        nc.sync.dma_start(dq_raw[:], dquery.rearrange("(p j) q -> p j q", j=PACK))
        for r in range(PACK):
            nc.sync.dma_start(key_bytes[r:P:QUADRANT, :].bitcast(I32), keys_scales[0, r:SCALE_ROWS:PACK, :].bitcast(I32))
        nc.sync.dma_start(key_words[:].bitcast(I32), keys_words[0].rearrange("p n t -> p (n t)").bitcast(I32))

        def load_values(block, slot):
            pool = in_slot(slot, [P, T], F32, f"vals{block}")
            nc.sync.dma_start(pool[:], vals[block * P : (block + 1) * P, :])
            return pool

        def quantize_rows(raw, name, round_rows):
            rounded = in_slot("slot_" + name + "_rounded", [P, Q, PACK], BF16, name + "_rounded")
            round_rows(rounded[:].rearrange("p (c i) j -> p c j i", i=LINE), raw[:].rearrange("p j (c i) -> p c j i", i=LINE))
            codes = aligned([P, Q], U32, name + "_codes")
            scales = aligned([P, Q], U8, name + "_scales")
            quantize(codes[:], scales[:], rounded[:].rearrange("p q j -> p (q j)"))
            return codes, scales

        got_bytes = aligned([P, SLOTS], U8, "got_bytes")
        nc.vector.tensor_copy(got_bytes[:], key_bytes[:].indirect(offsets[:]))
        q_mx = quantize_rows(q_raw, "q", nc.vector.tensor_copy)
        vals2 = load_values(2, "slot_q")
        dq_mx = quantize_rows(dq_raw, "dq", lambda dst, src: nc.scalar.activation(dst, src, ACT.Copy))
        vals0 = load_values(0, "slot_dq")
        vals1 = load_values(1, "slot_dq_rounded")
        factor = in_slot("slot_q_rounded", [P, PACK], F32, "factor")
        nc.sync.dma_start(factor[:], slot_factor.rearrange("o (p t) -> p (o t)", t=PACK))

        got_words = aligned([P, SLOTS], U32, "got_words")
        scores = []
        for h in range(HALVES):
            cols = slice(h * HALF, (h + 1) * HALF)
            entries = offsets[:, h * HALF // PER_COLUMN : (h + 1) * HALF // PER_COLUMN]
            nc.vector.tensor_copy(got_words[:, cols], key_words[:].indirect(entries))
            bank = ps.tile([P, 2, HALF], F32, name=f"scores{h}", tag=f"scores{h}")
            for plane, (codes, scales) in enumerate((q_mx, dq_mx)):
                multiply(bank[:, plane, :], codes[:], scales[:], got_words[:, cols], got_bytes[:, cols])
            scores.append(bank)
        vals3 = load_values(3, "slot_keys")

        def dealt(half_plane):
            return half_plane.rearrange("p (m t) -> p t m", t=PACK)

        sums = in_slot("slot_sums", [P, 2, SPANS], F32, "sums")
        sig = sb.tile([P, PACK, P], F32, name="sig")
        dealt_half = [slice(h * P // HALVES, (h + 1) * P // HALVES) for h in range(HALVES)]
        for h in range(HALVES):
            nc.vector.tensor_reduce(
                sums[:, :, h * SPANS // HALVES : (h + 1) * SPANS // HALVES],
                scores[h][:].rearrange("p c (g s) -> p c g s", s=SPAN), AXIS.X, ALU.add,
            )
            nc.scalar.activation(sig[:, :, dealt_half[h]], dealt(scores[h][:, 0, :]), ACT.Sigmoid)

        means = sb.tile([P, 2, SPANS], F32, name="means")
        nc.vector.tensor_scalar(means[:], sums[:], 1.0 / SPAN, None, ALU.mult)
        s_mean, ts = means[:, 0, :], means[:, 1, :]
        neg_max = in_slot("slot_scalar", [P, 1], F32, "neg_max")
        nc.vector.tensor_reduce(neg_max[:], s_mean, AXIS.X, ALU.max, negate=True)
        p = sb.tile([P, SPANS], F32, name="p")
        p_sum = sb.tile([P, 1], F32, name="p_sum")
        nc.scalar.activation(p[:], s_mean, ACT.Exp, bias=neg_max[:], accum_out=p_sum[:])

        neg_own = sb.tile([P, PACK, P], F32, name="neg_own")
        for h in range(HALVES):
            nc.vector.scalar_tensor_tensor(
                neg_own[:, :, dealt_half[h]], sig[:, :, dealt_half[h]], 1.0, dealt(scores[h][:, 1, :]), ALU.subtract, ALU.mult
            )

        def turn(got, bank_tag):
            pairs = got[:].bitcast(F32)
            turned = ps.tile([P, 2, P], F32, name="turned", tag=bank_tag)
            for u in range(2):
                nc.tensor.transpose(turned[:, u, :], pairs[:, u : SLOTS // 2 : 2], identity[:])
            return turned

        def weave(turned, woven):
            nc.scalar.copy(woven.bitcast(F32).rearrange("p (e u) -> p e u", u=2), turned[:].rearrange("p u e -> p e u"))

        def gather_values(pool, slot, bank_tag):
            got = in_slot(slot, [P, SLOTS], BF16, "got_" + bank_tag)
            nc.vector.tensor_copy(got[:], pool[:].indirect(offsets[:]))
            return turn(got, bank_tag)

        turned0 = gather_values(vals0, "slot_sums", "turned0")

        rows = in_slot("slot_dq", [P, SPANS + 2 * BLOCK32], F32, "rows")
        tp, inv_sum, tp_sum = rows[:, 0:SPANS], rows[:, SPANS : SPANS + 1], rows[:, SPANS + BLOCK32 : SPANS + BLOCK32 + 1]
        nc.vector.reciprocal(inv_sum, p_sum[:])
        nc.vector.scalar_tensor_tensor(tp, p[:], 1.0, ts, ALU.mult, ALU.mult, accum_out=tp_sum)

        shares = in_slot("slot_shares", [P, P + BLOCK32], F32, "shares")
        neg_share, mean = shares[:, 0:P], shares[:, P : P + 1]

        def by_column(per_span):
            return per_span.unsqueeze(2).to_broadcast([P, SPANS, SPAN_PARTS])

        nc.vector.tensor_scalar(neg_share.rearrange("p (g h) -> p g h", h=SPAN_PARTS), by_column(p[:]), inv_sum, -1.0, ALU.mult, ALU.mult)
        nc.vector.tensor_scalar(mean, tp_sum, inv_sum, None, ALU.mult)
        neg_gate = sb.tile([P, PACK, P], F32, name="neg_gate")
        nc.vector.tensor_tensor(neg_gate[:], sig[:], neg_share.unsqueeze(1).to_broadcast([P, PACK, P]), ALU.mult)
        neg_span = sb.tile([P, SPANS, SPAN_PARTS], F32, name="neg_span")
        nc.vector.tensor_scalar(neg_span[:], by_column(ts), mean, -1.0, ALU.subtract, ALU.mult)

        neg_gate_t = ps.tile([P, PACK, Q], F32, name="neg_gate_t", tag="scores0")
        neg_bracket_t = ps.tile([P, PACK, Q], F32, name="neg_bracket_t")
        for t in range(PACK):
            nc.tensor.transpose(neg_gate_t[:, t, :], neg_gate[:, t, :], identity[:])
        for t in range(PACK):
            nc.tensor.matmul(neg_bracket_t[:, t, :], neg_own[:, t, :], identity[:], start=True, stop=False, is_transpose=True)
            nc.tensor.matmul(
                neg_bracket_t[:, t, :], neg_span[:].rearrange("p g h -> p (g h)"), identity[:], start=False, stop=True, is_transpose=True
            )
        turned1 = gather_values(vals1, "slot_got1", "turned1")

        rounded2 = in_slot("slot_scalar", [P, T], BF16, "rounded2")
        nc.scalar.activation(rounded2[:], vals2[:], ACT.Copy)
        got2 = in_slot("slot_got2", [P, SLOTS], BF16, "got2")
        nc.scalar.activation(got2[:], rounded2[:].indirect(offsets[:]), ACT.Copy)
        turned2 = turn(got2, "turned23")
        neg_factor = in_slot("slot_scalar", [P, PACK, Q], F32, "neg_factor")
        for t in range(PACK):
            nc.scalar.activation(neg_factor[:, t, :], neg_gate_t[:, t, :], ACT.Copy, scale=factor[:, t : t + 1])
        woven2 = aligned([P, P * PACK], BF16, "woven2")
        weave(turned2, woven2[:])
        woven01 = in_slot("slot_got2", [P, PAIR * PACK], BF16, "woven01")
        weave(turned0, woven01[:, 0 : P * PACK])
        weave(turned1, woven01[:, P * PACK : PAIR * PACK])
        turned3 = gather_values(vals3, "slot_shares", "turned23")
        woven3 = aligned([P, P * PACK], BF16, "woven3")
        weave(turned3, woven3[:])

        w_rounded = in_slot("slot_keys", [P, Q, PACK], BF16, "w_rounded")
        nc.vector.tensor_tensor(
            w_rounded[:].rearrange("p (c i) t -> p c t i", i=LINE),
            neg_bracket_t[:].rearrange("p t (c i) -> p c t i", i=LINE),
            neg_factor[:].rearrange("p t (c i) -> p c t i", i=LINE), ALU.mult,
        )
        v_codes = in_slot("slot_scalar", [P, E - P], U32, "v_codes")
        v_scales = aligned([P, E - P], U8, "v_scales")
        v3_codes = aligned([P, P], U32, "v3_codes")
        v3_scales = aligned([P, P], U8, "v3_scales")
        w_codes = aligned([P, Q], U32, "w_codes")
        w_scales = aligned([P, Q], U8, "w_scales")
        quantize(v_codes[:, PAIR : E - P], v_scales[:, PAIR : E - P], woven2[:])
        quantize(w_codes[:], w_scales[:], w_rounded[:].rearrange("p q t -> p (q t)"))
        quantize(v_codes[:, 0:PAIR], v_scales[:, 0:PAIR], woven01[:])
        quantize(v3_codes[:], v3_scales[:], woven3[:])

        low = ps.tile([P, PAIR], F32, name="low", tag="scores1")
        high = ps.tile([P, PAIR], F32, name="high")
        multiply(high[:, 0:P], w_codes[:], w_scales[:], v_codes[:, PAIR : E - P], v_scales[:, PAIR : E - P])
        multiply(low[:], w_codes[:], w_scales[:], v_codes[:, 0:PAIR], v_scales[:, 0:PAIR])
        multiply(high[:, P:PAIR], w_codes[:], w_scales[:], v3_codes[:], v3_scales[:])
        out_low = sb.tile([P, PAIR], F32, name="out_low")
        nc.scalar.copy(out_low[:], low[:])
        nc.sync.dma_start(out[:, 0:PAIR], out_low[:])
        out_high = sb.tile([P, PAIR], F32, name="out_high")
        nc.vector.tensor_copy(out_high[:], high[:])
        nc.sync.dma_start(out[:, PAIR:E], out_high[:])
